import numpy as np
import ml_dtypes


def mxq(x, axis, fmt="e4m3"):
    dtype, down = {"e4m3": (ml_dtypes.float8_e4m3fn, 7), "e5m2": (ml_dtypes.float8_e5m2, 14)}[fmt]
    v = np.moveaxis(np.asarray(x, np.float32).astype(ml_dtypes.bfloat16).astype(np.float64), axis, -1)
    blocks = v.reshape(v.shape[:-1] + (-1, 32))
    amax = np.abs(blocks).max(-1, keepdims=True)
    byte = np.maximum(np.where(amax > 0, np.frexp(amax)[1] - 1 + 127, 0) - down, 1)
    scale = np.exp2(byte - 127.0)
    codes = (blocks / scale).astype(np.float32).astype(dtype).astype(np.float64)
    return np.moveaxis((codes * scale).reshape(v.shape), -1, axis)


WIDE = False


def mx_kscale(k):
    if not WIDE:
        return np.ones(k)
    levels = np.array([10, -10, 5, -5, 0])
    if k % 512:
        return np.exp2(np.random.permutation(np.resize(levels, k // 32))).repeat(32)
    a = np.empty((k // 512, 16))
    for p in range(k // 512):
        a[p, :8] = np.random.permutation(np.resize(levels, 8))
        for g in range(8):
            far = levels[np.abs(levels - a[p, g]) >= 10]
            a[p, g + 8] = far[np.random.randint(len(far))]
    return np.exp2(a.ravel()).repeat(32)


def f64(x):
    return np.asarray(x).astype(np.float64)


def striped(idx):
    return np.tile(idx.reshape(-1, 16).T, (8, 1)).astype(np.uint16)


def unstriped(offs):
    return offs[:16].T.reshape(-1).astype(np.int64)


E2M1 = np.array([0.0, 0.5, 1.0, 1.5, 2.0, 3.0, 4.0, 6.0, -0.0, -0.5, -1.0, -1.5, -2.0, -3.0, -4.0, -6.0])


def pack_weight(w, fmt):
    k, n = w.shape
    w = f64(np.asarray(w, np.float32).astype(ml_dtypes.bfloat16)).reshape(k // 32, 32, n)
    amax = np.abs(w).max(1)
    if fmt == "e4m3":
        byte = np.frexp(amax)[1] - 1 + 127 - 7
    else:
        mant, ex = np.frexp(amax / 6.0)
        byte = np.where(mant > 0.5, ex, ex - 1) + 127
    byte = np.clip(np.where(amax > 0, byte, 1), 1, 254)
    scaled = (w * np.exp2(127.0 - byte)[:, None, :]).reshape(k, n).astype(np.float32)
    by_word = np.ascontiguousarray(scaled.reshape(k // 512, 128, 4, n).transpose(0, 1, 3, 2))
    if fmt == "e4m3":
        words = by_word.astype(ml_dtypes.float8_e4m3fn).view(np.uint8)
    else:
        c = by_word.astype(ml_dtypes.float4_e2m1fn).view(np.uint8) & 0xF
        words = (c[..., 0::2] | (c[..., 1::2] << 4)).reshape(k // 512, 128, 2 * n)
    return np.ascontiguousarray(words), np.ascontiguousarray(byte.astype(np.uint8).reshape(k // 512, 16, n))


def unpack_weight(words, scales, fmt):
    g, _, n = scales.shape
    words = np.ascontiguousarray(words).reshape(g, 128, n, -1)
    if fmt == "e4m3":
        vals = words.view(ml_dtypes.float8_e4m3fn).astype(np.float64)
    else:
        nib = np.empty((g, 128, n, 4), np.uint8)
        nib[..., 0::2] = words & 0xF
        nib[..., 1::2] = words >> 4
        vals = E2M1[nib]
    vals = vals * np.repeat(np.exp2(scales.astype(np.float64) - 127.0), 8, axis=1)[..., None]
    return vals.transpose(0, 1, 3, 2).reshape(g * 512, n)


def gelu(v):
    return 0.5 * v * (1.0 + np.tanh(np.sqrt(2.0 / np.pi) * (v + 0.044715 * v**3)))


def striped8(idx):
    return np.concatenate([v.reshape(-1, 16).T for v in idx]).astype(np.uint16)


def unstriped8(offs):
    return np.stack([offs[16 * g:16 * g + 16].T.reshape(-1) for g in range(8)]).astype(np.int64)


def runs(v, idx8):
    k = np.arange(v.shape[0])
    return v[k[:, None], idx8[k % 512 // 64]]


K, T, S, H, P, N = 1024, 2048, 1024, 1024, 512, 384


def setup_inputs():
    n = np.random.standard_normal
    s = mx_kscale(K)[:, None]
    u = mx_kscale(H)[:, None]
    d = {}
    d["tab_words"], d["tab_scales"] = pack_weight(n((K, T)) * s, "e4m3")
    d["offs"] = striped8(np.stack([np.random.permutation(T)[:S] for _ in range(8)]))
    d["pos1"] = striped(np.random.permutation(S)[:P])
    d["pos2"] = striped(np.random.permutation(S)[:P])
    d["w1"] = (1.5 * n((K, H)) / K**0.5 / s).astype(np.float32)
    d["gain"] = (1.2 * np.exp(0.3 * n(H)) * u[:, 0]).astype(np.float32)
    d["w2_words"], d["w2_scales"] = pack_weight(0.8 * n((K, H)) / K**0.5 / s * u.T, "e2m1")
    d["mat"] = np.exp(0.5 * n((H, P))).astype(np.float32)
    d["w3_words"], d["w3_scales"] = pack_weight(0.7 * n((H, N)) / H**0.5 / u, "e4m3")
    d["bo"] = (0.5 * n(N)).astype(np.float32)
    return d


def reference(tab_words, tab_scales, offs, pos1, pos2, w1, gain, w2_words, w2_scales, mat, w3_words, w3_scales, bo):
    v = runs(unpack_weight(tab_words, tab_scales, "e4m3"), unstriped8(offs))
    w1q = mxq(f64(w1), 0, "e4m3")
    w2 = unpack_weight(w2_words, w2_scales, "e2m1")
    w3 = unpack_weight(w3_words, w3_scales, "e4m3")
    a = w1q.T @ v
    act = 0.5 * a * (1.0 + np.tanh(0.7978845608 * (a + 0.044715 * a**3)))
    b = w2.T @ v
    h = f64(gain)[:, None] * act - b
    z = f64(mat) * h[:, unstriped(pos1)] - h[:, unstriped(pos2)]
    y = w3.T @ mxq(z, 0, "e4m3")
    return y + f64(bo)[:, None]

@@ -1,0 +1,309 @@
+from contextlib import ExitStack
+
+import concourse.mybir as mybir
+
+K, T, S, H, PAIRS, N = 1024, 2048, 1024, 1024, 512, 384
+FLOPS = 2 * 2 * K * H * S + 2 * H * N * PAIRS
+
+F32 = mybir.dt.float32
+BF16 = mybir.dt.bfloat16
+I32 = mybir.dt.int32
+U32 = mybir.dt.uint32
+U16 = mybir.dt.uint16
+U8 = mybir.dt.uint8
+FP8X4 = mybir.dt.float8_e4m3fn_x4
+FP4X4 = mybir.dt.float4_e2m1fn_x4
+ALU = mybir.AluOpType
+ACT = mybir.ActivationFunctionType
+
+P = 128
+PACK = 4
+PASS = P * PACK
+BANK = 512
+HALF = PAIRS // 2
+ROW_TILES = H // P
+N_TILES = N // P
+
+
+def tile_list_banknote_zone_scores_kernel(
+    tc, tab_words, tab_scales, offs, pos1, pos2, w1, gain, w2_words, w2_scales, mat, w3_words, w3_scales, bo, out
+):
+    nc = tc.nc
+    with ExitStack() as ctx:
+        lists = ctx.enter_context(tc.tile_pool(name="lists", bufs=1))
+        keep = ctx.enter_context(tc.tile_pool(name="keep", bufs=1))
+        ring = ctx.enter_context(tc.tile_pool(name="ring", bufs=3))
+        psum = ctx.enter_context(tc.psum_pool(name="psum", bufs=4))
+
+        def kept(shape, dtype, name, tag=None):
+            return keep.tile(shape, dtype, name=name, tag=tag or name, align_bytes=64)
+
+        offs_t = lists.tile([P, S // 16], U16, name="offs_t")
+        pos1_t = lists.tile([P, PAIRS // 16], U16, name="pos1_t")
+        pos2_t = lists.tile([P, PAIRS // 16], U16, name="pos2_t")
+        nc.sync.dma_start(offs_t[:], offs)
+        nc.sync.dma_start(pos1_t[:], pos1)
+        nc.sync.dma_start(pos2_t[:], pos2)
+
+        tab_sc = kept([P, T], U8, "tab_sc")
+        w_sc = kept([P, 2 * H], U8, "w_sc")
+        planes = [kept([P, S], U8, "plane%d" % a) for a in range(2)]
+        warm = kept([P, 2], F32, "warm")
+        nc.vector.memset(tab_sc[:].bitcast(I32), 0)
+        nc.vector.memset(w_sc[:].bitcast(I32), 0)
+        nc.vector.memset(planes[1][:].bitcast(I32), 0)
+        nc.vector.memset(warm[:, 0:1], 0.0)
+        nc.scalar.activation(warm[:, 1:2], warm[:, 0:1], ACT.Gelu_apprx_tanh)
+
+        def load_tab(a):
+            t = kept([P, T], I32, "tab%d" % a)
+            nc.sync.dma_start(t[:], tab_words[a].rearrange("p t i -> p (t i)").bitcast(I32))
+            return t
+
+        def load_w1(a, b):
+            t = kept([P, PACK, PASS], F32, "w1raw%d%d" % (a, b), tag="w1raw%d" % a)
+            rows = w1[a * PASS : (a + 1) * PASS, b * PASS : (b + 1) * PASS]
+            nc.sync.dma_start(t[:], rows.rearrange("(p j) c -> p j c", j=PACK))
+            return t
+
+        def load_w2(b, tag):
+            t = kept([P, 2, 2 * PASS], U8, "w2raw%d" % b, tag=tag)
+            src = w2_words.rearrange("a p c -> p a c")[:, :, 2 * PASS * b : 2 * PASS * (b + 1)]
+            nc.sync.dma_start(t[:].bitcast(I32), src.bitcast(I32))
+            return t
+
+        def load_scale_rows(dst, src, width):
+            for d in range(4):
+                rows = dst[:, 0 : 2 * width].bitcast(I32)[32 * d : 32 * d + 4, :]
+                nc.sync.dma_start(
+                    rows.rearrange("p (a w) -> p a w", a=2),
+                    src[:, 4 * d : 4 * d + 4, :].rearrange("a j c -> j a c").bitcast(I32),
+                )
+
+        def load_mat(b):
+            t = kept([P, PACK, PAIRS], F32, "mat%d" % b, tag="tab%d" % b)
+            nc.sync.dma_start(t[:], mat[b * PASS : (b + 1) * PASS, :].rearrange("(p t) m -> p t m", t=PACK))
+            return t
+
+        tab = [load_tab(0), None]
+        for a in range(2):
+            for e in range(2):
+                nc.sync.dma_start(
+                    tab_sc[:].bitcast(I32)[8 * a + e : P : 16, :],
+                    tab_scales[a].rearrange("(g e) t -> e g t", e=2)[e].bitcast(I32),
+                )
+        w2raw = [load_w2(0, "w2raw0"), None]
+        w1raw = {(0, 0): load_w1(0, 0), (1, 0): load_w1(1, 0)}
+        load_scale_rows(w_sc, w2_scales, H)
+        tab[1] = load_tab(1)
+
+        w2q, w2s, w1q, w1s = {}, {}, {}, {}
+
+        def deal_w2_words(b):
+            t = kept([P, 2 * 2 * PASS], U8, "w2q%d" % b)
+            nc.vector.tensor_copy(
+                t[:].bitcast(U16).rearrange("p (a t q) -> p a t q", a=2, t=PACK),
+                w2raw[b][:].bitcast(U16).rearrange("p a (q t) -> p a t q", t=PACK),
+            )
+            w2q[b] = t
+
+        def deal_w2_scales(b):
+            t = kept([P, 2 * PASS], U8, "w2s%d" % b)
+            nc.vector.tensor_copy(
+                t[:].rearrange("p (a t q) -> p a t q", a=2, t=PACK),
+                w_sc[:].rearrange("p (a b q t) -> p b a t q", a=2, b=2, t=PACK)[:, b],
+            )
+            w2s[b] = t
+
+        grouped = {}
+
+        def cast_w1(a, b):
+            g = kept([P, PACK * PASS], BF16, "w1g%d%d" % (a, b), tag="w1g%d" % a)
+            dst = g[:].rearrange("p (t m j) -> p m j t", t=PACK, j=PACK)
+            src = w1raw[a, b][:].rearrange("p j (m t) -> p m j t", t=PACK)
+            for u in range(2):
+                ms = slice(u * P // 2, (u + 1) * P // 2)
+                nc.scalar.copy(dst[:, ms], src[:, ms])
+            grouped[a, b] = g
+
+        def quantize_w1(a, b):
+            w1q[a, b] = kept([P, PASS], U32, "w1q%d%d" % (a, b))
+            w1s[a, b] = kept([P, PASS], U8, "w1s%d%d" % (a, b))
+            nc.vector.quantize_mx(out=w1q[a, b][:].bitcast(FP8X4), scales=w1s[a, b][:], in_=grouped[a, b][:])
+
+        vq = {}
+
+        def gather_words(a, hf):
+            vq[a, hf] = kept([P, BANK], U32, "vq%d%d" % (a, hf))
+            cols = slice(hf * BANK // 16, (hf + 1) * BANK // 16)
+            nc.vector.tensor_copy(vq[a, hf][:], tab[a][:].bitcast(U32).indirect(offs_t[:, cols]))
+
+        picked = kept([P, S], U8, "picked", tag="late")
+        nc.vector.tensor_copy(picked[:], tab_sc[:].indirect(offs_t[:]))
+        nc.vector.tensor_copy(planes[0][:].bitcast(I32), picked[:].bitcast(I32))
+        for a in range(2):
+            for j in range(2 * (1 - a), 4):
+                nc.sync.dma_start(
+                    planes[a][:].bitcast(I32)[j:P:32, :],
+                    picked[:].bitcast(I32)[16 * (j // 2) + 8 * a + j % 2 : P : 32, :],
+                )
+
+        gain_t = kept([P, 2, PACK], F32, "gain_t", tag="tab_sc")
+        nc.sync.dma_start(gain_t[:], gain.rearrange("(b p t) -> p b t", b=2, t=PACK))
+
+        deal_w2_words(0)
+        gather_words(0, 0)
+        gather_words(0, 1)
+        mats = [load_mat(0), None]
+        cast_w1(0, 0)
+        cast_w1(1, 0)
+        deal_w2_scales(0)
+        quantize_w1(0, 0)
+        gather_words(1, 0)
+        quantize_w1(1, 0)
+        gather_words(1, 1)
+        w1raw[0, 1] = load_w1(0, 1)
+        w1raw[1, 1] = load_w1(1, 1)
+        w2raw[1] = load_w2(1, "late")
+        mats[1] = load_mat(1)
+
+        banks, hs, t1s = {}, {}, {}
+
+        def one_pass(i, hf, kind, a):
+            b, t = divmod(i, PACK)
+            cols = slice(t * P, (t + 1) * P)
+            if kind == 0:
+                lhsT, lhsT_scale = w1q[a, b][:, cols].bitcast(FP8X4), w1s[a, b][:, cols]
+            else:
+                c0 = a * PASS + t * P
+                lhsT, lhsT_scale = w2q[b][:, 2 * c0 : 2 * (c0 + P)].bitcast(FP4X4), w2s[b][:, c0 : c0 + P]
+            nc.tensor.matmul_mx(
+                out=banks[i, hf, kind][:],
+                lhsT=lhsT,
+                lhsT_scale=lhsT_scale,
+                rhs=vq[a, hf][:].bitcast(FP8X4),
+                rhs_scale=planes[a][:, hf * BANK : (hf + 1) * BANK],
+                start=(a == 0),
+                stop=(a == 1),
+            )
+
+        def products(i):
+            for hf in range(2):
+                for kind in range(2):
+                    banks[i, hf, kind] = psum.tile([P, BANK], F32, name="acc%d" % kind)
+            if i == 0:
+                order = [(hf, kind, a) for a in range(2) for hf in range(2) for kind in range(2)]
+            else:
+                order = [(hf, kind, a) for hf in range(2) for kind in range(2) for a in range(2)]
+            for hf, kind, a in order:
+                one_pass(i, hf, kind, a)
+
+        def combine(i, hf):
+            b, t = divmod(i, PACK)
+            if hf == 0:
+                hs[i] = ring.tile([P, S], F32, name="h")
+            act = ring.tile([P, BANK], F32, name="act")
+            nc.scalar.activation(act[:], banks[i, hf, 0][:], ACT.Gelu_apprx_tanh)
+            nc.vector.scalar_tensor_tensor(
+                hs[i][:, hf * BANK : (hf + 1) * BANK],
+                act[:],
+                gain_t[:, b, t : t + 1],
+                banks[i, hf, 1][:],
+                ALU.mult,
+                ALU.subtract,
+            )
+
+        zneg = [kept([P, PACK, PAIRS], F32, "zneg%d" % b) for b in range(2)]
+
+        def pick_front(i):
+            b, t = divmod(i, PACK)
+            t1s[i] = ring.tile([P, PAIRS], F32, name="front")
+            nc.vector.tensor_tensor(t1s[i][:], hs[i][:].indirect(pos1_t[:]), mats[b][:, t, :], ALU.mult)
+
+        def pick_back(i, c0, c1):
+            b, t = divmod(i, PACK)
+            nc.vector.tensor_tensor(
+                zneg[b][:, t, c0:c1], hs[i][:].indirect(pos2_t[:, c0 // 16 : c1 // 16]), t1s[i][:, c0:c1], ALU.subtract
+            )
+
+        zb, zq, zs = {}, {}, {}
+
+        def cast_z(b, hf, copy):
+            zb[b, hf] = kept([P, PACK * HALF], BF16, "zb%d%d" % (b, hf))
+            src = zneg[b][:, :, hf * HALF : (hf + 1) * HALF]
+            copy(
+                zb[b, hf][:].rearrange("p (c i t) -> p c t i", i=4, t=PACK),
+                src.rearrange("p t (c i) -> p c t i", i=4),
+            )
+
+        def quantize_z(b, hf):
+            zq[b, hf] = kept([P, HALF], U32, "zq%d%d" % (b, hf))
+            zs[b, hf] = kept([P, HALF], U8, "zs%d%d" % (b, hf))
+            nc.vector.quantize_mx(out=zq[b, hf][:].bitcast(FP8X4), scales=zs[b, hf][:], in_=zb[b, hf][:])
+
+        products(0)
+        combine(0, 0)
+        combine(0, 1)
+        last = ROW_TILES - 1
+        for i in range(last):
+            products(i + 1)
+            combine(i + 1, 0)
+            pick_front(i)
+            combine(i + 1, 1)
+            pick_back(i, 0, PAIRS)
+            if i == 0:
+                cast_w1(0, 1)
+                deal_w2_words(1)
+                deal_w2_scales(1)
+                w3q = kept([P, 2, N], I32, "w3q", tag="late")
+                nc.sync.dma_start(w3q[:], w3_words.rearrange("a p c i -> p a (c i)").bitcast(I32))
+                load_scale_rows(w_sc, w3_scales, N)
+            if i == 1:
+                cast_w1(1, 1)
+                quantize_w1(0, 1)
+                quantize_w1(1, 1)
+                bo_t = kept([P, N_TILES], F32, "bo_t", tag="w1g1")
+                with nc.allow_non_contiguous_dma(reason="one bias value for each partition"):
+                    nc.sync.dma_start(bo_t[:], bo.rearrange("(t p) -> p t", p=P))
+            if i == PACK - 1:
+                for hf in range(2):
+                    cast_z(0, hf, nc.scalar.copy)
+            if i == PACK:
+                for hf in range(2):
+                    quantize_z(0, hf)
+
+        ys = {}
+
+        def score_pass(b, hf):
+            for nt in range(N_TILES):
+                if b == 0:
+                    ys[hf, nt] = psum.tile([P, HALF], F32, name="acc%d" % hf)
+                nc.tensor.matmul_mx(
+                    out=ys[hf, nt][:],
+                    lhsT=w3q[:, b, nt * P : (nt + 1) * P].bitcast(FP8X4),
+                    lhsT_scale=w_sc[:, b * N + nt * P : b * N + (nt + 1) * P],
+                    rhs=zq[b, hf][:].bitcast(FP8X4),
+                    rhs_scale=zs[b, hf][:],
+                    start=(b == 0),
+                    stop=(b == 1),
+                )
+
+        pick_front(last)
+        for hf in range(2):
+            score_pass(0, hf)
+        pick_back(last, 0, HALF)
+        pick_back(last, HALF, PAIRS)
+        cast_z(1, 0, nc.scalar.copy)
+        cast_z(1, 1, nc.vector.tensor_copy)
+        out_v = out.rearrange("(t p) m -> p t m", p=P)
+        for hf in range(2):
+            quantize_z(1, hf)
+        for hf in range(2):
+            score_pass(1, hf)
+            res = kept([P, N_TILES, HALF], F32, "res%d" % hf)
+            for nt in range(N_TILES):
+                if (hf + nt) % 2 == 0:
+                    nc.scalar.activation(res[:, nt, :], ys[hf, nt][:], ACT.Identity, bias=bo_t[:, nt : nt + 1], scale=-1.0)
+                else:
+                    nc.vector.tensor_scalar(res[:, nt, :], ys[hf, nt][:], -1.0, bo_t[:, nt : nt + 1], ALU.mult, ALU.add)
+            nc.sync.dma_start(out_v[:, :, hf * HALF : (hf + 1) * HALF], res[:])

@@ -41,9 +41,6 @@ def tile_list_banknote_zone_scores_kernel(
         offs_t = lists.tile([P, S // 16], U16, name="offs_t")
         pos1_t = lists.tile([P, PAIRS // 16], U16, name="pos1_t")
         pos2_t = lists.tile([P, PAIRS // 16], U16, name="pos2_t")
-        nc.sync.dma_start(offs_t[:], offs)
-        nc.sync.dma_start(pos1_t[:], pos1)
-        nc.sync.dma_start(pos2_t[:], pos2)
 
         tab_sc = kept([P, T], U8, "tab_sc")
         w_sc = kept([P, 2 * H], U8, "w_sc")
@@ -51,79 +48,80 @@ def tile_list_banknote_zone_scores_kernel(
         warm = kept([P, 2], F32, "warm")
         nc.vector.memset(tab_sc[:].bitcast(I32), 0)
         nc.vector.memset(w_sc[:].bitcast(I32), 0)
-        nc.vector.memset(planes[1][:].bitcast(I32), 0)
+        nc.vector.memset(planes[0][:].bitcast(I32), 0)
         nc.vector.memset(warm[:, 0:1], 0.0)
         nc.scalar.activation(warm[:, 1:2], warm[:, 0:1], ACT.Gelu_apprx_tanh)
 
+        tab, w1raw, mats = {}, {}, {}
+
         def load_tab(a):
-            t = kept([P, T], I32, "tab%d" % a)
-            nc.sync.dma_start(t[:], tab_words[a].rearrange("p t i -> p (t i)").bitcast(I32))
-            return t
+            tab[a] = kept([P, T], I32, "tab%d" % a)
+            nc.sync.dma_start(tab[a][:], tab_words[a].rearrange("p t i -> p (t i)").bitcast(I32))
 
-        def load_w1(a, b):
-            t = kept([P, PACK, PASS], F32, "w1raw%d%d" % (a, b), tag="w1raw%d" % a)
-            rows = w1[a * PASS : (a + 1) * PASS, b * PASS : (b + 1) * PASS]
-            nc.sync.dma_start(t[:], rows.rearrange("(p j) c -> p j c", j=PACK))
-            return t
+        def load_w1(a, b, pieces):
+            width = PASS // pieces
+            for u in range(pieces):
+                t = kept([P, PACK, width], F32, "w1raw%d%d%d" % (a, b, u))
+                c0 = b * PASS + u * width
+                rows = w1[a * PASS : (a + 1) * PASS, c0 : c0 + width]
+                nc.sync.dma_start(t[:], rows.rearrange("(p j) c -> p j c", j=PACK))
+                for v in range(2 // pieces):
+                    w1raw[a, b, u + v] = t[:, :, v * PASS // 2 : (v + 1) * PASS // 2]
 
-        def load_w2(b, tag):
-            t = kept([P, 2, 2 * PASS], U8, "w2raw%d" % b, tag=tag)
-            src = w2_words.rearrange("a p c -> p a c")[:, :, 2 * PASS * b : 2 * PASS * (b + 1)]
-            nc.sync.dma_start(t[:].bitcast(I32), src.bitcast(I32))
-            return t
-
-        def load_scale_rows(dst, src, width):
-            for d in range(4):
-                rows = dst[:, 0 : 2 * width].bitcast(I32)[32 * d : 32 * d + 4, :]
+        def load_scale_rows(src, width, quadrants):
+            for d in quadrants:
+                rows = w_sc[:, 0 : 2 * width].bitcast(I32)[32 * d : 32 * d + 4, :]
                 nc.sync.dma_start(
                     rows.rearrange("p (a w) -> p a w", a=2),
                     src[:, 4 * d : 4 * d + 4, :].rearrange("a j c -> j a c").bitcast(I32),
                 )
 
-        def load_mat(b):
-            t = kept([P, PACK, PAIRS], F32, "mat%d" % b, tag="tab%d" % b)
-            nc.sync.dma_start(t[:], mat[b * PASS : (b + 1) * PASS, :].rearrange("(p t) m -> p t m", t=PACK))
-            return t
+        def load_mat(b, t0, t1):
+            tile = kept([P, t1 - t0, PAIRS], F32, "mat%d%d" % (b, t0))
+            rows = mat[b * PASS : (b + 1) * PASS, :].rearrange("(p t) m -> p t m", t=PACK)
+            nc.sync.dma_start(tile[:], rows[:, t0:t1, :])
+            for t in range(t0, t1):
+                mats[b, t] = tile[:, t - t0, :]
 
-        tab = [load_tab(0), None]
+        w2raw = kept([P, 2, 2 * H], U8, "w2raw")
+        nc.sync.dma_start(w2raw[:].bitcast(I32), w2_words.rearrange("a p c -> p a c").bitcast(I32))
         for a in range(2):
             for e in range(2):
                 nc.sync.dma_start(
-                    tab_sc[:].bitcast(I32)[8 * a + e : P : 16, :],
+                    tab_sc[:].bitcast(I32)[8 * (1 - a) + e : P : 16, :],
                     tab_scales[a].rearrange("(g e) t -> e g t", e=2)[e].bitcast(I32),
                 )
-        w2raw = [load_w2(0, "w2raw0"), None]
-        w1raw = {(0, 0): load_w1(0, 0), (1, 0): load_w1(1, 0)}
-        load_scale_rows(w_sc, w2_scales, H)
-        tab[1] = load_tab(1)
+        nc.sync.dma_start(offs_t[:], offs)
+        load_scale_rows(w2_scales, H, range(0, 1))
+        load_w1(0, 0, 1)
+        load_scale_rows(w2_scales, H, range(1, 4))
+        load_tab(0)
+        load_w1(1, 0, 2)
 
-        w2q, w2s, w1q, w1s = {}, {}, {}, {}
+        w1q, w1s = {}, {}
+        w2q = kept([P, 2 * 2 * H], U8, "w2q")
+        w2s = kept([P, 2 * H], U8, "w2s")
 
-        def deal_w2_words(b):
-            t = kept([P, 2 * 2 * PASS], U8, "w2q%d" % b)
+        def deal_w2_words():
             nc.vector.tensor_copy(
-                t[:].bitcast(U16).rearrange("p (a t q) -> p a t q", a=2, t=PACK),
-                w2raw[b][:].bitcast(U16).rearrange("p a (q t) -> p a t q", t=PACK),
+                w2q[:].bitcast(U16).rearrange("p (g t q) -> p g t q", g=4, t=PACK),
+                w2raw[:].bitcast(U16).rearrange("p a (b q t) -> p (a b) t q", b=2, t=PACK),
             )
-            w2q[b] = t
 
-        def deal_w2_scales(b):
-            t = kept([P, 2 * PASS], U8, "w2s%d" % b)
+        def deal_w2_scales():
             nc.vector.tensor_copy(
-                t[:].rearrange("p (a t q) -> p a t q", a=2, t=PACK),
-                w_sc[:].rearrange("p (a b q t) -> p b a t q", a=2, b=2, t=PACK)[:, b],
+                w2s[:].rearrange("p (g t q) -> p g t q", g=4, t=PACK),
+                w_sc[:].rearrange("p (g q t) -> p g t q", g=4, t=PACK),
             )
-            w2s[b] = t
 
         grouped = {}
 
         def cast_w1(a, b):
-            g = kept([P, PACK * PASS], BF16, "w1g%d%d" % (a, b), tag="w1g%d" % a)
+            g = kept([P, PACK * PASS], BF16, "w1g%d%d" % (a, b))
             dst = g[:].rearrange("p (t m j) -> p m j t", t=PACK, j=PACK)
-            src = w1raw[a, b][:].rearrange("p j (m t) -> p m j t", t=PACK)
             for u in range(2):
-                ms = slice(u * P // 2, (u + 1) * P // 2)
-                nc.scalar.copy(dst[:, ms], src[:, ms])
+                src = w1raw[a, b, u].rearrange("p j (m t) -> p m j t", t=PACK)
+                nc.scalar.copy(dst[:, u * P // 2 : (u + 1) * P // 2], src)
             grouped[a, b] = g
 
         def quantize_w1(a, b):
@@ -138,34 +136,47 @@ def tile_list_banknote_zone_scores_kernel(
             cols = slice(hf * BANK // 16, (hf + 1) * BANK // 16)
             nc.vector.tensor_copy(vq[a, hf][:], tab[a][:].bitcast(U32).indirect(offs_t[:, cols]))
 
-        picked = kept([P, S], U8, "picked", tag="late")
-        nc.vector.tensor_copy(picked[:], tab_sc[:].indirect(offs_t[:]))
-        nc.vector.tensor_copy(planes[0][:].bitcast(I32), picked[:].bitcast(I32))
-        for a in range(2):
-            for j in range(2 * (1 - a), 4):
+        picked = kept([P, S], U8, "picked")
+
+        def move_rows(a, js):
+            for j in js:
                 nc.sync.dma_start(
                     planes[a][:].bitcast(I32)[j:P:32, :],
-                    picked[:].bitcast(I32)[16 * (j // 2) + 8 * a + j % 2 : P : 32, :],
+                    picked[:].bitcast(I32)[16 * (j // 2) + 8 * (1 - a) + j % 2 : P : 32, :],
                 )
 
-        gain_t = kept([P, 2, PACK], F32, "gain_t", tag="tab_sc")
+        deal_w2_words()
+        nc.vector.tensor_copy(picked[:], tab_sc[:].indirect(offs_t[:]))
+        move_rows(0, range(4))
+        load_tab(1)
+        nc.vector.tensor_copy(planes[1][:].bitcast(I32), picked[:].bitcast(I32))
+        move_rows(1, range(2, 4))
+        load_mat(0, 0, 2)
+        gain_t = kept([P, 2, PACK], F32, "gain_t")
         nc.sync.dma_start(gain_t[:], gain.rearrange("(b p t) -> p b t", b=2, t=PACK))
+        nc.sync.dma_start(pos1_t[:], pos1)
+        nc.sync.dma_start(pos2_t[:], pos2)
+        load_w1(0, 1, 1)
+        load_w1(1, 1, 1)
+        load_mat(0, 2, 4)
+        load_mat(1, 0, 4)
 
-        deal_w2_words(0)
+        deal_w2_scales()
+        cast_w1(0, 0)
+        quantize_w1(0, 0)
         gather_words(0, 0)
         gather_words(0, 1)
-        mats = [load_mat(0), None]
-        cast_w1(0, 0)
         cast_w1(1, 0)
-        deal_w2_scales(0)
-        quantize_w1(0, 0)
-        gather_words(1, 0)
         quantize_w1(1, 0)
+        gather_words(1, 0)
         gather_words(1, 1)
-        w1raw[0, 1] = load_w1(0, 1)
-        w1raw[1, 1] = load_w1(1, 1)
-        w2raw[1] = load_w2(1, "late")
-        mats[1] = load_mat(1)
+
+        load_scale_rows(w3_scales, N, range(4))
+        w3q = kept([P, 2, N], I32, "w3q")
+        nc.sync.dma_start(w3q[:], w3_words.rearrange("a p c i -> p a (c i)").bitcast(I32))
+        bo_t = kept([P, N_TILES], F32, "bo_t")
+        with nc.allow_non_contiguous_dma(reason="one bias value for each partition"):
+            nc.sync.dma_start(bo_t[:], bo.rearrange("(t p) -> p t", p=P))
 
         banks, hs, t1s = {}, {}, {}
 
@@ -175,8 +186,8 @@ def tile_list_banknote_zone_scores_kernel(
             if kind == 0:
                 lhsT, lhsT_scale = w1q[a, b][:, cols].bitcast(FP8X4), w1s[a, b][:, cols]
             else:
-                c0 = a * PASS + t * P
-                lhsT, lhsT_scale = w2q[b][:, 2 * c0 : 2 * (c0 + P)].bitcast(FP4X4), w2s[b][:, c0 : c0 + P]
+                c0 = a * H + b * PASS + t * P
+                lhsT, lhsT_scale = w2q[:, 2 * c0 : 2 * (c0 + P)].bitcast(FP4X4), w2s[:, c0 : c0 + P]
             nc.tensor.matmul_mx(
                 out=banks[i, hf, kind][:],
                 lhsT=lhsT,
@@ -187,16 +198,15 @@ def tile_list_banknote_zone_scores_kernel(
                 stop=(a == 1),
             )
 
-        def products(i):
-            for hf in range(2):
-                for kind in range(2):
-                    banks[i, hf, kind] = psum.tile([P, BANK], F32, name="acc%d" % kind)
-            if i == 0:
-                order = [(hf, kind, a) for a in range(2) for hf in range(2) for kind in range(2)]
-            else:
-                order = [(hf, kind, a) for hf in range(2) for kind in range(2) for a in range(2)]
-            for hf, kind, a in order:
-                one_pass(i, hf, kind, a)
+        def open_banks(i, hf):
+            for kind in range(2):
+                banks[i, hf, kind] = psum.tile([P, BANK], F32, name="acc%d" % kind)
+
+        def products(i, hf):
+            open_banks(i, hf)
+            for kind in range(2):
+                for a in range(2):
+                    one_pass(i, hf, kind, a)
 
         def combine(i, hf):
             b, t = divmod(i, PACK)
@@ -215,10 +225,13 @@ def tile_list_banknote_zone_scores_kernel(
 
         zneg = [kept([P, PACK, PAIRS], F32, "zneg%d" % b) for b in range(2)]
 
-        def pick_front(i):
+        def pick_front(i, c0, c1):
             b, t = divmod(i, PACK)
-            t1s[i] = ring.tile([P, PAIRS], F32, name="front")
-            nc.vector.tensor_tensor(t1s[i][:], hs[i][:].indirect(pos1_t[:]), mats[b][:, t, :], ALU.mult)
+            if c0 == 0:
+                t1s[i] = ring.tile([P, PAIRS], F32, name="front")
+            nc.vector.tensor_tensor(
+                t1s[i][:, c0:c1], hs[i][:].indirect(pos1_t[:, c0 // 16 : c1 // 16]), mats[b, t][:, c0:c1], ALU.mult
+            )
 
         def pick_back(i, c0, c1):
             b, t = divmod(i, PACK)
@@ -241,30 +254,28 @@ def tile_list_banknote_zone_scores_kernel(
             zs[b, hf] = kept([P, HALF], U8, "zs%d%d" % (b, hf))
             nc.vector.quantize_mx(out=zq[b, hf][:].bitcast(FP8X4), scales=zs[b, hf][:], in_=zb[b, hf][:])
 
-        products(0)
-        combine(0, 0)
-        combine(0, 1)
+        first = [(i, hf) for hf in range(2) for i in range(2)]
+        for i, hf in first:
+            open_banks(i, hf)
+        for a in range(2):
+            for i, hf in first:
+                for kind in range(2):
+                    one_pass(i, hf, kind, a)
+        for i, hf in first[:3]:
+            combine(i, hf)
         last = ROW_TILES - 1
         for i in range(last):
-            products(i + 1)
-            combine(i + 1, 0)
-            pick_front(i)
+            pick_front(i, 0, PAIRS)
+            if i > 0:
+                products(i + 1, 1)
             combine(i + 1, 1)
             pick_back(i, 0, PAIRS)
-            if i == 0:
-                cast_w1(0, 1)
-                deal_w2_words(1)
-                deal_w2_scales(1)
-                w3q = kept([P, 2, N], I32, "w3q", tag="late")
-                nc.sync.dma_start(w3q[:], w3_words.rearrange("a p c i -> p a (c i)").bitcast(I32))
-                load_scale_rows(w_sc, w3_scales, N)
-            if i == 1:
-                cast_w1(1, 1)
-                quantize_w1(0, 1)
-                quantize_w1(1, 1)
-                bo_t = kept([P, N_TILES], F32, "bo_t", tag="w1g1")
-                with nc.allow_non_contiguous_dma(reason="one bias value for each partition"):
-                    nc.sync.dma_start(bo_t[:], bo.rearrange("(t p) -> p t", p=P))
+            if i + 2 <= last:
+                products(i + 2, 0)
+                combine(i + 2, 0)
+            if i < 2:
+                cast_w1(i, 1)
+                quantize_w1(i, 1)
             if i == PACK - 1:
                 for hf in range(2):
                     cast_z(0, hf, nc.scalar.copy)
@@ -288,7 +299,8 @@ def tile_list_banknote_zone_scores_kernel(
                     stop=(b == 1),
                 )
 
-        pick_front(last)
+        pick_front(last, 0, HALF)
+        pick_front(last, HALF, PAIRS)
         for hf in range(2):
             score_pass(0, hf)
         pick_back(last, 0, HALF)

from contextlib import ExitStack

import concourse.mybir as mybir

K, T, S, H, PAIRS, N = 1024, 2048, 1024, 1024, 512, 384
FLOPS = 2 * 2 * K * H * S + 2 * H * N * PAIRS

F32 = mybir.dt.float32
BF16 = mybir.dt.bfloat16
I32 = mybir.dt.int32
U32 = mybir.dt.uint32
U16 = mybir.dt.uint16
U8 = mybir.dt.uint8
FP8X4 = mybir.dt.float8_e4m3fn_x4
FP4X4 = mybir.dt.float4_e2m1fn_x4
ALU = mybir.AluOpType
ACT = mybir.ActivationFunctionType

P = 128
PACK = 4
PASS = P * PACK
BANK = 512
HALF = PAIRS // 2
ROW_TILES = H // P
N_TILES = N // P


def tile_list_banknote_zone_scores_kernel(
    tc, tab_words, tab_scales, offs, pos1, pos2, w1, gain, w2_words, w2_scales, mat, w3_words, w3_scales, bo, out
):
    nc = tc.nc
    with ExitStack() as ctx:
        lists = ctx.enter_context(tc.tile_pool(name="lists", bufs=1))
        keep = ctx.enter_context(tc.tile_pool(name="keep", bufs=1))
        ring = ctx.enter_context(tc.tile_pool(name="ring", bufs=3))
        psum = ctx.enter_context(tc.psum_pool(name="psum", bufs=4))

        def kept(shape, dtype, name, tag=None):
            return keep.tile(shape, dtype, name=name, tag=tag or name, align_bytes=64)

        offs_t = lists.tile([P, S // 16], U16, name="offs_t")
        pos1_t = lists.tile([P, PAIRS // 16], U16, name="pos1_t")
        pos2_t = lists.tile([P, PAIRS // 16], U16, name="pos2_t")

        tab_sc = kept([P, T], U8, "tab_sc")
        w_sc = kept([P, 2 * H], U8, "w_sc")
        planes = [kept([P, S], U8, "plane%d" % a) for a in range(2)]
        warm = kept([P, 2], F32, "warm")
        nc.vector.memset(tab_sc[:].bitcast(I32), 0)
        nc.vector.memset(w_sc[:].bitcast(I32), 0)
        nc.vector.memset(planes[0][:].bitcast(I32), 0)
        nc.vector.memset(warm[:, 0:1], 0.0)
        nc.scalar.activation(warm[:, 1:2], warm[:, 0:1], ACT.Gelu_apprx_tanh)

        tab, w1raw, mats = {}, {}, {}

        def load_tab(a):
            tab[a] = kept([P, T], I32, "tab%d" % a)
            nc.sync.dma_start(tab[a][:], tab_words[a].rearrange("p t i -> p (t i)").bitcast(I32))

        def load_w1(a, b, pieces):
            width = PASS // pieces
            for u in range(pieces):
                t = kept([P, PACK, width], F32, "w1raw%d%d%d" % (a, b, u))
                c0 = b * PASS + u * width
                rows = w1[a * PASS : (a + 1) * PASS, c0 : c0 + width]
                nc.sync.dma_start(t[:], rows.rearrange("(p j) c -> p j c", j=PACK))
                for v in range(2 // pieces):
                    w1raw[a, b, u + v] = t[:, :, v * PASS // 2 : (v + 1) * PASS // 2]

        def load_scale_rows(src, width, quadrants):
            for d in quadrants:
                rows = w_sc[:, 0 : 2 * width].bitcast(I32)[32 * d : 32 * d + 4, :]
                nc.sync.dma_start(
                    rows.rearrange("p (a w) -> p a w", a=2),
                    src[:, 4 * d : 4 * d + 4, :].rearrange("a j c -> j a c").bitcast(I32),
                )

        def load_mat(b, t0, t1):
            tile = kept([P, t1 - t0, PAIRS], F32, "mat%d%d" % (b, t0))
            rows = mat[b * PASS : (b + 1) * PASS, :].rearrange("(p t) m -> p t m", t=PACK)
            nc.sync.dma_start(tile[:], rows[:, t0:t1, :])
            for t in range(t0, t1):
                mats[b, t] = tile[:, t - t0, :]

        w2raw = kept([P, 2, 2 * H], U8, "w2raw")
        nc.sync.dma_start(w2raw[:].bitcast(I32), w2_words.rearrange("a p c -> p a c").bitcast(I32))
        for a in range(2):
            for e in range(2):
                nc.sync.dma_start(
                    tab_sc[:].bitcast(I32)[8 * (1 - a) + e : P : 16, :],
                    tab_scales[a].rearrange("(g e) t -> e g t", e=2)[e].bitcast(I32),
                )
        nc.sync.dma_start(offs_t[:], offs)
        load_scale_rows(w2_scales, H, range(0, 1))
        load_w1(0, 0, 1)
        load_scale_rows(w2_scales, H, range(1, 4))
        load_tab(0)
        load_w1(1, 0, 2)

        w1q, w1s = {}, {}
        w2q = kept([P, 2 * 2 * H], U8, "w2q")
        w2s = kept([P, 2 * H], U8, "w2s")

        def deal_w2_words():
            nc.vector.tensor_copy(
                w2q[:].bitcast(U16).rearrange("p (g t q) -> p g t q", g=4, t=PACK),
                w2raw[:].bitcast(U16).rearrange("p a (b q t) -> p (a b) t q", b=2, t=PACK),
            )

        def deal_w2_scales():
            nc.vector.tensor_copy(
                w2s[:].rearrange("p (g t q) -> p g t q", g=4, t=PACK),
                w_sc[:].rearrange("p (g q t) -> p g t q", g=4, t=PACK),
            )

        grouped = {}

        def cast_w1(a, b):
            g = kept([P, PACK * PASS], BF16, "w1g%d%d" % (a, b))
            dst = g[:].rearrange("p (t m j) -> p m j t", t=PACK, j=PACK)
            for u in range(2):
                src = w1raw[a, b, u].rearrange("p j (m t) -> p m j t", t=PACK)
                nc.scalar.copy(dst[:, u * P // 2 : (u + 1) * P // 2], src)
            grouped[a, b] = g

        def quantize_w1(a, b):
            w1q[a, b] = kept([P, PASS], U32, "w1q%d%d" % (a, b))
            w1s[a, b] = kept([P, PASS], U8, "w1s%d%d" % (a, b))
            nc.vector.quantize_mx(out=w1q[a, b][:].bitcast(FP8X4), scales=w1s[a, b][:], in_=grouped[a, b][:])

        vq = {}

        def gather_words(a, hf):
            vq[a, hf] = kept([P, BANK], U32, "vq%d%d" % (a, hf))
            cols = slice(hf * BANK // 16, (hf + 1) * BANK // 16)
            nc.vector.tensor_copy(vq[a, hf][:], tab[a][:].bitcast(U32).indirect(offs_t[:, cols]))

        picked = kept([P, S], U8, "picked")

        def move_rows(a, js):
            for j in js:
                nc.sync.dma_start(
                    planes[a][:].bitcast(I32)[j:P:32, :],
                    picked[:].bitcast(I32)[16 * (j // 2) + 8 * (1 - a) + j % 2 : P : 32, :],
                )

        deal_w2_words()
        nc.vector.tensor_copy(picked[:], tab_sc[:].indirect(offs_t[:]))
        move_rows(0, range(4))
        load_tab(1)
        nc.vector.tensor_copy(planes[1][:].bitcast(I32), picked[:].bitcast(I32))
        move_rows(1, range(2, 4))
        load_mat(0, 0, 2)
        gain_t = kept([P, 2, PACK], F32, "gain_t")
        nc.sync.dma_start(gain_t[:], gain.rearrange("(b p t) -> p b t", b=2, t=PACK))
        nc.sync.dma_start(pos1_t[:], pos1)
        nc.sync.dma_start(pos2_t[:], pos2)
        load_w1(0, 1, 1)
        load_w1(1, 1, 1)
        load_mat(0, 2, 4)
        load_mat(1, 0, 4)

        deal_w2_scales()
        cast_w1(0, 0)
        quantize_w1(0, 0)
        gather_words(0, 0)
        gather_words(0, 1)
        cast_w1(1, 0)
        quantize_w1(1, 0)
        gather_words(1, 0)
        gather_words(1, 1)

        load_scale_rows(w3_scales, N, range(4))
        w3q = kept([P, 2, N], I32, "w3q")
        nc.sync.dma_start(w3q[:], w3_words.rearrange("a p c i -> p a (c i)").bitcast(I32))
        bo_t = kept([P, N_TILES], F32, "bo_t")
        with nc.allow_non_contiguous_dma(reason="one bias value for each partition"):
            nc.sync.dma_start(bo_t[:], bo.rearrange("(t p) -> p t", p=P))

        banks, hs, t1s = {}, {}, {}

        def one_pass(i, hf, kind, a):
            b, t = divmod(i, PACK)
            cols = slice(t * P, (t + 1) * P)
            if kind == 0:
                lhsT, lhsT_scale = w1q[a, b][:, cols].bitcast(FP8X4), w1s[a, b][:, cols]
            else:
                c0 = a * H + b * PASS + t * P
                lhsT, lhsT_scale = w2q[:, 2 * c0 : 2 * (c0 + P)].bitcast(FP4X4), w2s[:, c0 : c0 + P]
            nc.tensor.matmul_mx(
                out=banks[i, hf, kind][:],
                lhsT=lhsT,
                lhsT_scale=lhsT_scale,
                rhs=vq[a, hf][:].bitcast(FP8X4),
                rhs_scale=planes[a][:, hf * BANK : (hf + 1) * BANK],
                start=(a == 0),
                stop=(a == 1),
            )

        def open_banks(i, hf):
            for kind in range(2):
                banks[i, hf, kind] = psum.tile([P, BANK], F32, name="acc%d" % kind)

        def products(i, hf):
            open_banks(i, hf)
            for kind in range(2):
                for a in range(2):
                    one_pass(i, hf, kind, a)

        def combine(i, hf):
            b, t = divmod(i, PACK)
            if hf == 0:
                hs[i] = ring.tile([P, S], F32, name="h")
            act = ring.tile([P, BANK], F32, name="act")
            nc.scalar.activation(act[:], banks[i, hf, 0][:], ACT.Gelu_apprx_tanh)
            nc.vector.scalar_tensor_tensor(
                hs[i][:, hf * BANK : (hf + 1) * BANK],
                act[:],
                gain_t[:, b, t : t + 1],
                banks[i, hf, 1][:],
                ALU.mult,
                ALU.subtract,
            )

        zneg = [kept([P, PACK, PAIRS], F32, "zneg%d" % b) for b in range(2)]

        def pick_front(i, c0, c1):
            b, t = divmod(i, PACK)
            if c0 == 0:
                t1s[i] = ring.tile([P, PAIRS], F32, name="front")
            nc.vector.tensor_tensor(
                t1s[i][:, c0:c1], hs[i][:].indirect(pos1_t[:, c0 // 16 : c1 // 16]), mats[b, t][:, c0:c1], ALU.mult
            )

        def pick_back(i, c0, c1):
            b, t = divmod(i, PACK)
            nc.vector.tensor_tensor(
                zneg[b][:, t, c0:c1], hs[i][:].indirect(pos2_t[:, c0 // 16 : c1 // 16]), t1s[i][:, c0:c1], ALU.subtract
            )

        zb, zq, zs = {}, {}, {}

        def cast_z(b, hf, copy):
            zb[b, hf] = kept([P, PACK * HALF], BF16, "zb%d%d" % (b, hf))
            src = zneg[b][:, :, hf * HALF : (hf + 1) * HALF]
            copy(
                zb[b, hf][:].rearrange("p (c i t) -> p c t i", i=4, t=PACK),
                src.rearrange("p t (c i) -> p c t i", i=4),
            )

        def quantize_z(b, hf):
            zq[b, hf] = kept([P, HALF], U32, "zq%d%d" % (b, hf))
            zs[b, hf] = kept([P, HALF], U8, "zs%d%d" % (b, hf))
            nc.vector.quantize_mx(out=zq[b, hf][:].bitcast(FP8X4), scales=zs[b, hf][:], in_=zb[b, hf][:])

        first = [(i, hf) for hf in range(2) for i in range(2)]
        for i, hf in first:
            open_banks(i, hf)
        for a in range(2):
            for i, hf in first:
                for kind in range(2):
                    one_pass(i, hf, kind, a)
        for i, hf in first[:3]:
            combine(i, hf)
        last = ROW_TILES - 1
        for i in range(last):
            pick_front(i, 0, PAIRS)
            if i > 0:
                products(i + 1, 1)
            combine(i + 1, 1)
            pick_back(i, 0, PAIRS)
            if i + 2 <= last:
                products(i + 2, 0)
                combine(i + 2, 0)
            if i < 2:
                cast_w1(i, 1)
                quantize_w1(i, 1)
            if i == PACK - 1:
                for hf in range(2):
                    cast_z(0, hf, nc.scalar.copy)
            if i == PACK:
                for hf in range(2):
                    quantize_z(0, hf)

        ys = {}

        def score_pass(b, hf):
            for nt in range(N_TILES):
                if b == 0:
                    ys[hf, nt] = psum.tile([P, HALF], F32, name="acc%d" % hf)
                nc.tensor.matmul_mx(
                    out=ys[hf, nt][:],
                    lhsT=w3q[:, b, nt * P : (nt + 1) * P].bitcast(FP8X4),
                    lhsT_scale=w_sc[:, b * N + nt * P : b * N + (nt + 1) * P],
                    rhs=zq[b, hf][:].bitcast(FP8X4),
                    rhs_scale=zs[b, hf][:],
                    start=(b == 0),
                    stop=(b == 1),
                )

        pick_front(last, 0, HALF)
        pick_front(last, HALF, PAIRS)
        for hf in range(2):
            score_pass(0, hf)
        pick_back(last, 0, HALF)
        pick_back(last, HALF, PAIRS)
        cast_z(1, 0, nc.scalar.copy)
        cast_z(1, 1, nc.vector.tensor_copy)
        out_v = out.rearrange("(t p) m -> p t m", p=P)
        for hf in range(2):
            quantize_z(1, hf)
        for hf in range(2):
            score_pass(1, hf)
            res = kept([P, N_TILES, HALF], F32, "res%d" % hf)
            for nt in range(N_TILES):
                if (hf + nt) % 2 == 0:
                    nc.scalar.activation(res[:, nt, :], ys[hf, nt][:], ACT.Identity, bias=bo_t[:, nt : nt + 1], scale=-1.0)
                else:
                    nc.vector.tensor_scalar(res[:, nt, :], ys[hf, nt][:], -1.0, bo_t[:, nt : nt + 1], ALU.mult, ALU.add)
            nc.sync.dma_start(out_v[:, :, hf * HALF : (hf + 1) * HALF], res[:])
